import numpy as np
import ml_dtypes


def mxq(x, axis, fmt="e4m3"):
    dtype, down = {"e4m3": (ml_dtypes.float8_e4m3fn, 7), "e5m2": (ml_dtypes.float8_e5m2, 14)}[fmt]
    v = np.moveaxis(np.asarray(x, np.float32).astype(ml_dtypes.bfloat16).astype(np.float64), axis, -1)
    blocks = v.reshape(v.shape[:-1] + (-1, 32))
    amax = np.abs(blocks).max(-1, keepdims=True)
    byte = np.maximum(np.where(amax > 0, np.frexp(amax)[1] - 1 + 127, 0) - down, 1)
    scale = np.exp2(byte - 127.0)
    codes = (blocks / scale).astype(np.float32).astype(dtype).astype(np.float64)
    return np.moveaxis((codes * scale).reshape(v.shape), -1, axis)


WIDE = False


def mx_kscale(k):
    if not WIDE:
        return np.ones(k)
    levels = np.array([24, -24, 12, -12, 0])
    if k % 512:
        return np.exp2(np.random.permutation(np.resize(levels, k // 32))).repeat(32)
    a = np.empty((k // 512, 16))
    for p in range(k // 512):
        a[p, :8] = np.random.permutation(np.resize(levels, 8))
        for g in range(8):
            far = levels[np.abs(levels - a[p, g]) >= 10]
            a[p, g + 8] = far[np.random.randint(len(far))]
    return np.exp2(a.ravel()).repeat(32)


def f64(x):
    return np.asarray(x).astype(np.float64)


def striped(idx):
    return np.tile(idx.reshape(-1, 16).T, (8, 1)).astype(np.uint16)


def unstriped(offs):
    return offs[:16].T.reshape(-1).astype(np.int64)


E2M1 = np.array([0.0, 0.5, 1.0, 1.5, 2.0, 3.0, 4.0, 6.0, -0.0, -0.5, -1.0, -1.5, -2.0, -3.0, -4.0, -6.0])


def pack_weight(w, fmt):
    k, n = w.shape
    w = f64(np.asarray(w, np.float32).astype(ml_dtypes.bfloat16)).reshape(k // 32, 32, n)
    amax = np.abs(w).max(1)
    if fmt == "e4m3":
        byte = np.frexp(amax)[1] - 1 + 127 - 7
    else:
        mant, ex = np.frexp(amax / 6.0)
        byte = np.where(mant > 0.5, ex, ex - 1) + 127
    byte = np.clip(np.where(amax > 0, byte, 1), 1, 254)
    scaled = (w * np.exp2(127.0 - byte)[:, None, :]).reshape(k, n).astype(np.float32)
    by_word = np.ascontiguousarray(scaled.reshape(k // 512, 128, 4, n).transpose(0, 1, 3, 2))
    if fmt == "e4m3":
        words = by_word.astype(ml_dtypes.float8_e4m3fn).view(np.uint8)
    else:
        c = by_word.astype(ml_dtypes.float4_e2m1fn).view(np.uint8) & 0xF
        words = (c[..., 0::2] | (c[..., 1::2] << 4)).reshape(k // 512, 128, 2 * n)
    return np.ascontiguousarray(words), np.ascontiguousarray(byte.astype(np.uint8).reshape(k // 512, 16, n))


def unpack_weight(words, scales, fmt):
    g, _, n = scales.shape
    words = np.ascontiguousarray(words).reshape(g, 128, n, -1)
    if fmt == "e4m3":
        vals = words.view(ml_dtypes.float8_e4m3fn).astype(np.float64)
    else:
        nib = np.empty((g, 128, n, 4), np.uint8)
        nib[..., 0::2] = words & 0xF
        nib[..., 1::2] = words >> 4
        vals = E2M1[nib]
    vals = vals * np.repeat(np.exp2(scales.astype(np.float64) - 127.0), 8, axis=1)[..., None]
    return vals.transpose(0, 1, 3, 2).reshape(g * 512, n)


def pack_table4(v):
    words, scales = pack_weight(v, "e2m1")
    g, t = words.shape[0] // 2, v.shape[1]
    return np.ascontiguousarray(words.reshape(g, 2, 128, t, 2).transpose(0, 2, 3, 1, 4).reshape(g, 128, t, 4)), scales


def unpack_table4(words, scales):
    g, _, t, _ = words.shape
    return unpack_weight(words.reshape(g, 128, t, 2, 2).transpose(0, 3, 1, 2, 4).reshape(2 * g, 128, 2 * t), scales, "e2m1")


K, N, T, J = 1024, 512, 2048, 1024


def setup_inputs():
    n = np.random.standard_normal
    s = mx_kscale(K)[:, None]
    p_tab = pack_table4(n((K, T)) * s)
    p_tab2 = pack_table4(n((K, T)) * s)
    p_wr4 = pack_weight(n((K, N)) / np.sqrt(2 * K) / s, "e2m1")
    p_wi = pack_weight(n((K, N)) / np.sqrt(2 * K) / s, "e4m3")
    return {
        "tab_words": p_tab[0],
        "tab_scales": p_tab[1],
        "tab2_words": p_tab2[0],
        "tab2_scales": p_tab2[1],
        "wr4_words": p_wr4[0],
        "wr4_scales": p_wr4[1],
        "wrd": (0.4 * (n((K, N)) / np.sqrt(2 * K) / s)).astype(np.float32),
        "wi_words": p_wi[0],
        "wi_scales": p_wi[1],
        "gT": (n((N, T))).astype(np.float32),
        "offs": striped(np.random.permutation(T)[:J]),
    }


def reference(tab_words, tab_scales, tab2_words, tab2_scales, wr4_words, wr4_scales, wrd, wi_words, wi_scales, gT, offs):
    idx = unstriped(offs)
    tab_ = unpack_table4(tab_words, tab_scales)[:, idx]
    tab2_ = unpack_table4(tab2_words, tab2_scales)[:, idx]
    wr4_ = unpack_weight(wr4_words, wr4_scales, "e2m1")
    wrd_ = mxq(f64(wrd), 0, "e4m3")
    wi_ = unpack_weight(wi_words, wi_scales, "e4m3")
    rr = wr4_.T @ tab_ + wrd_.T @ tab_
    ii = wi_.T @ tab2_
    zr = rr - ii
    ri = wr4_.T @ tab2_ + wrd_.T @ tab2_ + wi_.T @ tab_
    zi = ri
    return zr * f64(gT)[:, idx], zi * f64(gT)[:, idx]

@@ -1,0 +1,207 @@
+from contextlib import ExitStack
+
+import concourse.mybir as mybir
+
+K, N, T, J = 1024, 512, 2048, 1024
+FLOPS = 6 * 2 * K * N * J
+
+F32 = mybir.dt.float32
+BF16 = mybir.dt.bfloat16
+I32 = mybir.dt.int32
+U32 = mybir.dt.uint32
+U16 = mybir.dt.uint16
+U8 = mybir.dt.uint8
+FP8X4 = mybir.dt.float8_e4m3fn_x4
+FP4X4 = mybir.dt.float4_e2m1fn_x4
+MULT = mybir.AluOpType.mult
+SUB = mybir.AluOpType.subtract
+
+P = 128
+PASSES = 2
+HALF = 512
+HALVES = J // HALF
+ROW_TILES = N // P
+LIST_COLS = HALF // 16
+
+
+def tile_list_cpxtab_dl_gate_kernel(
+    tc, tab_words, tab_scales, tab2_words, tab2_scales, wr4_words, wr4_scales,
+    wrd, wi_words, wi_scales, gT, offs, out_0, out_1,
+):
+    nc = tc.nc
+    with ExitStack() as ctx:
+        keep = ctx.enter_context(tc.tile_pool(name="keep", bufs=1))
+        ring = ctx.enter_context(tc.tile_pool(name="ring", bufs=5))
+        psum3 = ctx.enter_context(tc.psum_pool(name="psum3", bufs=3))
+        psum2 = ctx.enter_context(tc.psum_pool(name="psum2", bufs=2))
+
+        staged = ctx.enter_context(tc.tile_pool(name="staged", bufs=1))
+        offsets = keep.tile([P, J // 16], U16, name="offsets")
+
+        words_hbm = (tab_words, tab2_words)
+        scales_hbm = (tab_scales, tab2_scales)
+        warm = keep.tile([P, 16], F32, name="warm")
+        word_win = [staged.tile([P, T], I32, name="word_win%d" % v, align_bytes=64, offset=8192 * v) for v in range(2)]
+        scale_win = [keep.tile([P, T], U8, name="scale_win%d" % v, align_bytes=64) for v in range(2)]
+        wr4_sc = keep.tile([P, PASSES, N], U8, name="wr4_sc", align_bytes=64)
+        wi_sc = keep.tile([P, PASSES, N], U8, name="wi_sc", align_bytes=64)
+        wr4_sb = staged.tile([P, PASSES, 2 * N], U8, name="wr4_sb", align_bytes=64, offset=16384)
+        wi_sb = staged.tile([P, PASSES, N], I32, name="wi_sb", align_bytes=64, offset=18432)
+        plane0 = {}
+        plane1 = [keep.tile([P, J], U8, name="plane1_%d" % v, align_bytes=64) for v in range(2)]
+        parted = [[keep.tile([P, PASSES, 2 * HALF], U8, name="parted%d_%d" % (v, h), align_bytes=64) for h in range(HALVES)] for v in range(2)]
+
+        nc.vector.memset(scale_win[0][:].bitcast(I32), 0)
+        nc.vector.memset(warm[:, 0:1], 0.0)
+        nc.scalar.copy(warm[:, 8:9], warm[:, 0:1])
+        nc.vector.memset(scale_win[1][:].bitcast(I32), 0)
+        nc.gpsimd.memset(wi_sc[:].bitcast(I32), 0)
+        nc.vector.memset(wr4_sc[:].bitcast(I32), 0)
+        for v in range(2):
+            nc.vector.memset(plane1[v][:].bitcast(I32), 0)
+
+        def load_scales(v):
+            for q in range(4):
+                nc.sync.dma_start(scale_win[v][32 * q : 32 * q + 8, :].bitcast(I32),
+                                  scales_hbm[v][:, 4 * q : 4 * q + 4, :].bitcast(I32))
+
+        def load_words(v):
+            nc.sync.dma_start(word_win[v][:], words_hbm[v][0].rearrange("p t b -> p (t b)").bitcast(I32))
+
+        def load_weight_scales(queue, dst, src):
+            for q in range(4):
+                queue.dma_start(dst[32 * q : 32 * q + 4, :, :].bitcast(I32),
+                                    src[:, 4 * q : 4 * q + 4, :].rearrange("a r n -> r a n").bitcast(I32))
+
+        wrd_raw = {}
+        gate_win = {}
+
+        def load_wrd(pair, a):
+            raw = staged.tile([P, 4, 2 * P], F32, name="wrd_raw%d_%d" % (pair, a), align_bytes=64, offset=22528 + 4096 * (2 * pair + a))
+            nc.sync.dma_start(raw[:], wrd[512 * a : 512 * (a + 1), 2 * P * pair : 2 * P * (pair + 1)].rearrange("(p i) n -> p i n", i=4))
+            wrd_raw[pair, a] = raw
+
+        def load_gate(n):
+            win = staged.tile([P, T], F32, name="gate_win%d" % n, align_bytes=64, offset=38912 + 8192 * n)
+            nc.sync.dma_start(win[:], gT[P * n : P * (n + 1), :])
+            gate_win[n] = win
+
+        def list_half(h):
+            return offsets[:, LIST_COLS * h : LIST_COLS * (h + 1)]
+
+        def gather_scales(v, h):
+            nc.vector.tensor_copy(plane0[v][:, HALF * h : HALF * (h + 1)], scale_win[v][:].indirect(list_half(h)))
+
+        def shift_scales(v):
+            nc.sync.dma_start(plane1[v][0:112, :].bitcast(I32), plane0[v][4:116, :].bitcast(I32))
+
+        def gather_words(v, h, picked):
+            nc.vector.tensor_copy(picked[:], word_win[v][:].bitcast(U32).indirect(list_half(h)))
+            return picked
+
+        def part_words(v, h, picked):
+            nc.vector.tensor_copy(parted[v][h][:].bitcast(U16), picked[:].bitcast(U16).rearrange("p (j a) -> p a j", a=PASSES))
+
+        def picked_tile(name, tag):
+            return keep.tile([P, HALF], U32, name=name, tag=tag, align_bytes=64)
+
+        wrd_codes = {}
+        wrd_sc = {}
+
+        def quantize_wrd(n):
+            grouped = keep.tile([P, PASSES, P, 4], BF16, name="grouped%d" % n, align_bytes=64)
+            for a in range(PASSES):
+                src = wrd_raw[n // 2, a][:, :, P * (n % 2) : P * (n % 2 + 1)]
+                nc.scalar.copy(grouped[:, a].rearrange("p (c x) i -> p c i x", x=4),
+                               src.rearrange("p i (c x) -> p c i x", x=4))
+            codes = keep.tile([P, PASSES * P], U32, name="wrd_codes%d" % n, align_bytes=64)
+            sc = keep.tile([P, PASSES * P], U8, name="wrd_sc%d" % n, align_bytes=64)
+            nc.vector.quantize_mx(out=codes[:].bitcast(FP8X4), scales=sc[:], in_=grouped[:].rearrange("p a c i -> p (a c i)"))
+            wrd_codes[n] = codes
+            wrd_sc[n] = sc
+
+        def weight(name, n, a):
+            if name == "wr4":
+                return wr4_sb[:, a, 2 * P * n : 2 * P * (n + 1)].bitcast(FP4X4), wr4_sc[:, a, P * n : P * (n + 1)]
+            if name == "wi":
+                return wi_sb[:, a, P * n : P * (n + 1)].bitcast(FP8X4), wi_sc[:, a, P * n : P * (n + 1)]
+            return wrd_codes[n][:, P * a : P * (a + 1)].bitcast(FP8X4), wrd_sc[n][:, P * a : P * (a + 1)]
+
+        def product(acc, steps, n, h):
+            for s, (name, v, a) in enumerate(steps):
+                w, w_sc = weight(name, n, a)
+                nc.tensor.matmul_mx(
+                    out=acc[:], lhsT=w, lhsT_scale=w_sc,
+                    rhs=parted[v][h][:, a, :].bitcast(FP4X4),
+                    rhs_scale=(plane0, plane1)[a][v][:, HALF * h : HALF * (h + 1)],
+                    start=(s == 0), stop=(s == len(steps) - 1),
+                )
+
+        def unit(n, h, evacuate, ii_sb, gate):
+            rr = psum3.tile([P, HALF], F32, name="rr")
+            ri = psum3.tile([P, HALF], F32, name="ri")
+            ii = psum2.tile([P, HALF], F32, name="ii")
+            product(rr, [("wr4", 0, 0), ("wr4", 0, 1), ("wrd", 0, 0), ("wrd", 0, 1)], n, h)
+            product(ii, [("wi", 1, 0), ("wi", 1, 1)], n, h)
+            product(ri, [("wi", 0, 0), ("wi", 0, 1), ("wr4", 1, 0), ("wr4", 1, 1), ("wrd", 1, 0), ("wrd", 1, 1)], n, h)
+            nc.scalar.copy(ii_sb[:], ii[:])
+            if evacuate:
+                rr_sb = ring.tile([P, HALF], F32, name="rr_sb")
+                ri_sb = ring.tile([P, HALF], F32, name="ri_sb")
+                nc.scalar.copy(rr_sb[:], rr[:])
+                nc.scalar.copy(ri_sb[:], ri[:])
+                rr, ri = rr_sb, ri_sb
+            nc.vector.tensor_copy(gate[:], gate_win[n][:].indirect(list_half(h)))
+            zr = ring.tile([P, HALF], F32, name="zr")
+            o0 = ring.tile([P, HALF], F32, name="o0")
+            o1 = ring.tile([P, HALF], F32, name="o1")
+            rows, cols = slice(P * n, P * (n + 1)), slice(HALF * h, HALF * (h + 1))
+            nc.vector.tensor_tensor(zr[:], rr[:], ii_sb[:], SUB)
+            nc.vector.tensor_tensor(o1[:], ri[:], gate[:], MULT)
+            nc.sync.dma_start(out_1[rows, cols], o1[:])
+            nc.vector.tensor_tensor(o0[:], zr[:], gate[:], MULT)
+            nc.sync.dma_start(out_0[rows, cols], o0[:])
+
+        plane0[0] = keep.tile([P, J], U8, name="plane0_0", align_bytes=64)
+        plane0[1] = keep.tile([P, J], U8, name="plane0_1", align_bytes=64)
+        load_words(0)
+        nc.sync.dma_start(offsets[:], offs)
+        load_scales(0)
+        nc.sync.dma_start(wr4_sb[:].bitcast(I32), wr4_words.rearrange("a p b -> p a b").bitcast(I32))
+        nc.sync.dma_start(wi_sb[:], wi_words.rearrange("a p n i -> p a (n i)").bitcast(I32))
+        load_weight_scales(nc.gpsimd, wi_sc, wi_scales)
+        load_scales(1)
+        load_words(1)
+        load_weight_scales(nc.sync, wr4_sc, wr4_scales)
+        picked00 = gather_words(0, 0, picked_tile("picked00", "slot_a"))
+        gather_scales(0, 0)
+        part_words(0, 0, picked00)
+        gather_scales(0, 1)
+        shift_scales(0)
+        load_wrd(0, 0)
+        load_wrd(0, 1)
+        gather_scales(1, 0)
+        gather_scales(1, 1)
+        shift_scales(1)
+        picked10 = gather_words(1, 0, picked_tile("picked10", "slot_b"))
+        part_words(1, 0, picked10)
+        load_gate(0)
+        load_wrd(1, 0)
+        load_wrd(1, 1)
+        load_gate(1)
+        load_gate(2)
+        load_gate(3)
+        quantize_wrd(0)
+        picked01 = gather_words(0, 1, picked_tile("picked01", "slot_b"))
+        quantize_wrd(1)
+        picked11 = gather_words(1, 1, staged.tile([P, HALF], U32, name="picked11", align_bytes=64, offset=0))
+        part_words(0, 1, picked01)
+        part_words(1, 1, picked11)
+        order = [(n, h) for h in range(HALVES) for n in range(ROW_TILES)]
+        for u, (n, h) in enumerate(order):
+            if u == 2:
+                quantize_wrd(2)
+                quantize_wrd(3)
+            ii_sb = staged.tile([P, HALF], F32, name="ii_sb%d" % u, align_bytes=64, offset=22528 + 2048 * (u % 4))
+            gate = staged.tile([P, HALF], F32, name="gate%d" % u, align_bytes=64, offset=71680 + 2048 * (u % 2))
+            unit(n, h, u < 6, ii_sb, gate)

@@ -31,8 +31,8 @@ def tile_list_cpxtab_dl_gate_kernel(
     nc = tc.nc
     with ExitStack() as ctx:
         keep = ctx.enter_context(tc.tile_pool(name="keep", bufs=1))
-        ring = ctx.enter_context(tc.tile_pool(name="ring", bufs=5))
-        psum3 = ctx.enter_context(tc.psum_pool(name="psum3", bufs=3))
+        ring = ctx.enter_context(tc.tile_pool(name="ring", bufs=4))
+        psum4 = ctx.enter_context(tc.psum_pool(name="psum4", bufs=4))
         psum2 = ctx.enter_context(tc.psum_pool(name="psum2", bufs=2))
 
         staged = ctx.enter_context(tc.tile_pool(name="staged", bufs=1))
@@ -41,12 +41,12 @@ def tile_list_cpxtab_dl_gate_kernel(
         words_hbm = (tab_words, tab2_words)
         scales_hbm = (tab_scales, tab2_scales)
         warm = keep.tile([P, 16], F32, name="warm")
-        word_win = [staged.tile([P, T], I32, name="word_win%d" % v, align_bytes=64, offset=8192 * v) for v in range(2)]
-        scale_win = [keep.tile([P, T], U8, name="scale_win%d" % v, align_bytes=64) for v in range(2)]
+        word_win = [staged.tile([P, T], I32, name="word_win%d" % v, align_bytes=64, offset=(16384, 24576)[v]) for v in range(2)]
+        scale_win = [staged.tile([P, T], U8, name="scale_win%d" % v, align_bytes=64, offset=(32768, 7168)[v]) for v in range(2)]
         wr4_sc = keep.tile([P, PASSES, N], U8, name="wr4_sc", align_bytes=64)
         wi_sc = keep.tile([P, PASSES, N], U8, name="wi_sc", align_bytes=64)
-        wr4_sb = staged.tile([P, PASSES, 2 * N], U8, name="wr4_sb", align_bytes=64, offset=16384)
-        wi_sb = staged.tile([P, PASSES, N], I32, name="wi_sb", align_bytes=64, offset=18432)
+        wr4_sb = staged.tile([P, PASSES, 2 * N], U8, name="wr4_sb", align_bytes=64, offset=51200)
+        wi_sb = staged.tile([P, PASSES, N], I32, name="wi_sb", align_bytes=64, offset=53248)
         plane0 = {}
         plane1 = [keep.tile([P, J], U8, name="plane1_%d" % v, align_bytes=64) for v in range(2)]
         parted = [[keep.tile([P, PASSES, 2 * HALF], U8, name="parted%d_%d" % (v, h), align_bytes=64) for h in range(HALVES)] for v in range(2)]
@@ -76,13 +76,13 @@ def tile_list_cpxtab_dl_gate_kernel(
         wrd_raw = {}
         gate_win = {}
 
-        def load_wrd(pair, a):
-            raw = staged.tile([P, 4, 2 * P], F32, name="wrd_raw%d_%d" % (pair, a), align_bytes=64, offset=22528 + 4096 * (2 * pair + a))
-            nc.sync.dma_start(raw[:], wrd[512 * a : 512 * (a + 1), 2 * P * pair : 2 * P * (pair + 1)].rearrange("(p i) n -> p i n", i=4))
-            wrd_raw[pair, a] = raw
+        def load_wrd(a):
+            raw = keep.tile([P, 4, N], F32, name="wrd_raw%d" % a)
+            nc.sync.dma_start(raw[:], wrd[512 * a : 512 * (a + 1), :].rearrange("(p i) n -> p i n", i=4))
+            wrd_raw[a] = raw
 
         def load_gate(n):
-            win = staged.tile([P, T], F32, name="gate_win%d" % n, align_bytes=64, offset=38912 + 8192 * n)
+            win = staged.tile([P, T], F32, name="gate_win%d" % n, align_bytes=64, offset=8192 * n)
             nc.sync.dma_start(win[:], gT[P * n : P * (n + 1), :])
             gate_win[n] = win
 
@@ -102,30 +102,29 @@ def tile_list_cpxtab_dl_gate_kernel(
         def part_words(v, h, picked):
             nc.vector.tensor_copy(parted[v][h][:].bitcast(U16), picked[:].bitcast(U16).rearrange("p (j a) -> p a j", a=PASSES))
 
-        def picked_tile(name, tag):
-            return keep.tile([P, HALF], U32, name=name, tag=tag, align_bytes=64)
+        def picked_tile(name, offset):
+            return staged.tile([P, HALF], U32, name=name, align_bytes=64, offset=offset)
 
         wrd_codes = {}
         wrd_sc = {}
 
-        def quantize_wrd(n):
-            grouped = keep.tile([P, PASSES, P, 4], BF16, name="grouped%d" % n, align_bytes=64)
-            for a in range(PASSES):
-                src = wrd_raw[n // 2, a][:, :, P * (n % 2) : P * (n % 2 + 1)]
-                nc.scalar.copy(grouped[:, a].rearrange("p (c x) i -> p c i x", x=4),
-                               src.rearrange("p i (c x) -> p c i x", x=4))
-            codes = keep.tile([P, PASSES * P], U32, name="wrd_codes%d" % n, align_bytes=64)
-            sc = keep.tile([P, PASSES * P], U8, name="wrd_sc%d" % n, align_bytes=64)
-            nc.vector.quantize_mx(out=codes[:].bitcast(FP8X4), scales=sc[:], in_=grouped[:].rearrange("p a c i -> p (a c i)"))
-            wrd_codes[n] = codes
-            wrd_sc[n] = sc
+        def quantize_wrd(a, pair):
+            grouped = staged.tile([P, 2 * P, 4], BF16, name="grouped%d_%d" % (a, pair), align_bytes=64, offset=34816 + 2048 * (2 * a + pair))
+            src = wrd_raw[a][:, :, 2 * P * pair : 2 * P * (pair + 1)]
+            nc.scalar.copy(grouped[:].rearrange("p (c x) i -> p c i x", x=4), src.rearrange("p i (c x) -> p c i x", x=4))
+            codes = keep.tile([P, 2 * P], U32, name="wrd_codes%d_%d" % (a, pair), align_bytes=64)
+            sc = keep.tile([P, 2 * P], U8, name="wrd_sc%d_%d" % (a, pair), align_bytes=64)
+            nc.vector.quantize_mx(out=codes[:].bitcast(FP8X4), scales=sc[:], in_=grouped[:].rearrange("p c i -> p (c i)"))
+            wrd_codes[a, pair] = codes
+            wrd_sc[a, pair] = sc
 
         def weight(name, n, a):
             if name == "wr4":
                 return wr4_sb[:, a, 2 * P * n : 2 * P * (n + 1)].bitcast(FP4X4), wr4_sc[:, a, P * n : P * (n + 1)]
             if name == "wi":
                 return wi_sb[:, a, P * n : P * (n + 1)].bitcast(FP8X4), wi_sc[:, a, P * n : P * (n + 1)]
-            return wrd_codes[n][:, P * a : P * (a + 1)].bitcast(FP8X4), wrd_sc[n][:, P * a : P * (a + 1)]
+            cols = slice(P * (n % 2), P * (n % 2 + 1))
+            return wrd_codes[a, n // 2][:, cols].bitcast(FP8X4), wrd_sc[a, n // 2][:, cols]
 
         def product(acc, steps, n, h):
             for s, (name, v, a) in enumerate(steps):
@@ -137,30 +136,31 @@ def tile_list_cpxtab_dl_gate_kernel(
                     start=(s == 0), stop=(s == len(steps) - 1),
                 )
 
-        def unit(n, h, evacuate, ii_sb, gate):
-            rr = psum3.tile([P, HALF], F32, name="rr")
-            ri = psum3.tile([P, HALF], F32, name="ri")
+        def unit(n, h, last, gate):
+            rr = psum2.tile([P, HALF], F32, name="rr")
             ii = psum2.tile([P, HALF], F32, name="ii")
-            product(rr, [("wr4", 0, 0), ("wr4", 0, 1), ("wrd", 0, 0), ("wrd", 0, 1)], n, h)
+            ri = psum4.tile([P, HALF], F32, name="ri")
             product(ii, [("wi", 1, 0), ("wi", 1, 1)], n, h)
-            product(ri, [("wi", 0, 0), ("wi", 0, 1), ("wr4", 1, 0), ("wr4", 1, 1), ("wrd", 1, 0), ("wrd", 1, 1)], n, h)
+            product(rr, [("wr4", 0, 0), ("wr4", 0, 1), ("wrd", 0, 0), ("wrd", 0, 1)], n, h)
+            product(ri, [("wi", 0, 0), ("wi", 0, 1), ("wr4", 1, 0), ("wrd", 1, 0), ("wr4", 1, 1), ("wrd", 1, 1)], n, h)
+            ii_sb = ring.tile([P, HALF], F32, name="ii_sb")
             nc.scalar.copy(ii_sb[:], ii[:])
-            if evacuate:
-                rr_sb = ring.tile([P, HALF], F32, name="rr_sb")
-                ri_sb = ring.tile([P, HALF], F32, name="ri_sb")
-                nc.scalar.copy(rr_sb[:], rr[:])
-                nc.scalar.copy(ri_sb[:], ri[:])
-                rr, ri = rr_sb, ri_sb
-            nc.vector.tensor_copy(gate[:], gate_win[n][:].indirect(list_half(h)))
             zr = ring.tile([P, HALF], F32, name="zr")
             o0 = ring.tile([P, HALF], F32, name="o0")
             o1 = ring.tile([P, HALF], F32, name="o1")
             rows, cols = slice(P * n, P * (n + 1)), slice(HALF * h, HALF * (h + 1))
-            nc.vector.tensor_tensor(zr[:], rr[:], ii_sb[:], SUB)
+            nc.vector.tensor_copy(gate[:], gate_win[n][:].indirect(list_half(h)))
+            if last:
+                nc.vector.tensor_tensor(zr[:], rr[:], ii_sb[:], SUB)
+                nc.vector.tensor_tensor(o0[:], zr[:], gate[:], MULT)
+            else:
+                rr_sb = ring.tile([P, HALF], F32, name="rr_sb")
+                nc.scalar.copy(rr_sb[:], rr[:])
+                nc.gpsimd.tensor_tensor(zr[:], rr_sb[:], ii_sb[:], SUB)
+                nc.gpsimd.tensor_tensor(o0[:], zr[:], gate[:], MULT)
+            nc.sync.dma_start(out_0[rows, cols], o0[:])
             nc.vector.tensor_tensor(o1[:], ri[:], gate[:], MULT)
             nc.sync.dma_start(out_1[rows, cols], o1[:])
-            nc.vector.tensor_tensor(o0[:], zr[:], gate[:], MULT)
-            nc.sync.dma_start(out_0[rows, cols], o0[:])
 
         plane0[0] = keep.tile([P, J], U8, name="plane0_0", align_bytes=64)
         plane0[1] = keep.tile([P, J], U8, name="plane0_1", align_bytes=64)
@@ -172,36 +172,32 @@ def tile_list_cpxtab_dl_gate_kernel(
         load_weight_scales(nc.gpsimd, wi_sc, wi_scales)
         load_scales(1)
         load_words(1)
+        load_wrd(0)
         load_weight_scales(nc.sync, wr4_sc, wr4_scales)
-        picked00 = gather_words(0, 0, picked_tile("picked00", "slot_a"))
+        picked00 = gather_words(0, 0, picked_tile("picked00", 43008))
         gather_scales(0, 0)
         part_words(0, 0, picked00)
         gather_scales(0, 1)
         shift_scales(0)
-        load_wrd(0, 0)
-        load_wrd(0, 1)
+        load_wrd(1)
         gather_scales(1, 0)
         gather_scales(1, 1)
         shift_scales(1)
-        picked10 = gather_words(1, 0, picked_tile("picked10", "slot_b"))
-        part_words(1, 0, picked10)
         load_gate(0)
-        load_wrd(1, 0)
-        load_wrd(1, 1)
         load_gate(1)
+        picked10 = gather_words(1, 0, picked_tile("picked10", 45056))
+        part_words(1, 0, picked10)
+        quantize_wrd(0, 0)
+        quantize_wrd(0, 1)
+        picked01 = gather_words(0, 1, picked_tile("picked01", 45056))
         load_gate(2)
-        load_gate(3)
-        quantize_wrd(0)
-        picked01 = gather_words(0, 1, picked_tile("picked01", "slot_b"))
-        quantize_wrd(1)
-        picked11 = gather_words(1, 1, staged.tile([P, HALF], U32, name="picked11", align_bytes=64, offset=0))
+        quantize_wrd(1, 0)
+        quantize_wrd(1, 1)
         part_words(0, 1, picked01)
+        picked11 = gather_words(1, 1, picked_tile("picked11", 34816 + 2048 * 2))
+        load_gate(3)
         part_words(1, 1, picked11)
         order = [(n, h) for h in range(HALVES) for n in range(ROW_TILES)]
         for u, (n, h) in enumerate(order):
-            if u == 2:
-                quantize_wrd(2)
-                quantize_wrd(3)
-            ii_sb = staged.tile([P, HALF], F32, name="ii_sb%d" % u, align_bytes=64, offset=22528 + 2048 * (u % 4))
-            gate = staged.tile([P, HALF], F32, name="gate%d" % u, align_bytes=64, offset=71680 + 2048 * (u % 2))
-            unit(n, h, u < 6, ii_sb, gate)
+            gate = staged.tile([P, HALF], F32, name="gate%d" % u, align_bytes=64, offset=57344 + 2048 * (u % 3))
+            unit(n, h, u == len(order) - 1, gate)

@@ -42,13 +42,13 @@ def tile_list_cpxtab_dl_gate_kernel(
         scales_hbm = (tab_scales, tab2_scales)
         warm = keep.tile([P, 16], F32, name="warm")
         word_win = [staged.tile([P, T], I32, name="word_win%d" % v, align_bytes=64, offset=(16384, 24576)[v]) for v in range(2)]
-        scale_win = [staged.tile([P, T], U8, name="scale_win%d" % v, align_bytes=64, offset=(32768, 7168)[v]) for v in range(2)]
+        scale_win = [keep.tile([P, T], U8, name="scale_win%d" % v, align_bytes=64) for v in range(2)]
         wr4_sc = keep.tile([P, PASSES, N], U8, name="wr4_sc", align_bytes=64)
         wi_sc = keep.tile([P, PASSES, N], U8, name="wi_sc", align_bytes=64)
         wr4_sb = staged.tile([P, PASSES, 2 * N], U8, name="wr4_sb", align_bytes=64, offset=51200)
         wi_sb = staged.tile([P, PASSES, N], I32, name="wi_sb", align_bytes=64, offset=53248)
         plane0 = {}
-        plane1 = [keep.tile([P, J], U8, name="plane1_%d" % v, align_bytes=64) for v in range(2)]
+        plane1 = {(v, h): keep.tile([P, HALF], U8, name="plane1_%d_%d" % (v, h), align_bytes=64) for h in range(HALVES) for v in range(2)}
         parted = [[keep.tile([P, PASSES, 2 * HALF], U8, name="parted%d_%d" % (v, h), align_bytes=64) for h in range(HALVES)] for v in range(2)]
 
         nc.vector.memset(scale_win[0][:].bitcast(I32), 0)
@@ -57,8 +57,8 @@ def tile_list_cpxtab_dl_gate_kernel(
         nc.vector.memset(scale_win[1][:].bitcast(I32), 0)
         nc.gpsimd.memset(wi_sc[:].bitcast(I32), 0)
         nc.vector.memset(wr4_sc[:].bitcast(I32), 0)
-        for v in range(2):
-            nc.vector.memset(plane1[v][:].bitcast(I32), 0)
+        for plane in plane1:
+            nc.vector.memset(plane1[plane][:].bitcast(I32), 0)
 
         def load_scales(v):
             for q in range(4):
@@ -89,11 +89,12 @@ def tile_list_cpxtab_dl_gate_kernel(
         def list_half(h):
             return offsets[:, LIST_COLS * h : LIST_COLS * (h + 1)]
 
-        def gather_scales(v, h):
-            nc.vector.tensor_copy(plane0[v][:, HALF * h : HALF * (h + 1)], scale_win[v][:].indirect(list_half(h)))
+        def gather_scales(v, h, offset):
+            plane0[v, h] = staged.tile([P, HALF], U8, name="plane0_%d_%d" % (v, h), align_bytes=64, offset=offset)
+            nc.vector.tensor_copy(plane0[v, h][:], scale_win[v][:].indirect(list_half(h)))
 
-        def shift_scales(v):
-            nc.sync.dma_start(plane1[v][0:112, :].bitcast(I32), plane0[v][4:116, :].bitcast(I32))
+        def shift_scales(queue, v, h):
+            queue.dma_start(plane1[v, h][0:112, :].bitcast(I32), plane0[v, h][4:116, :].bitcast(I32))
 
         def gather_words(v, h, picked):
             nc.vector.tensor_copy(picked[:], word_win[v][:].bitcast(U32).indirect(list_half(h)))
@@ -132,72 +133,67 @@ def tile_list_cpxtab_dl_gate_kernel(
                 nc.tensor.matmul_mx(
                     out=acc[:], lhsT=w, lhsT_scale=w_sc,
                     rhs=parted[v][h][:, a, :].bitcast(FP4X4),
-                    rhs_scale=(plane0, plane1)[a][v][:, HALF * h : HALF * (h + 1)],
+                    rhs_scale=(plane0, plane1)[a][v, h][:],
                     start=(s == 0), stop=(s == len(steps) - 1),
                 )
 
-        def unit(n, h, last, gate):
+        def unit(n, h, gating_engine, ii_sb, gate):
             rr = psum2.tile([P, HALF], F32, name="rr")
             ii = psum2.tile([P, HALF], F32, name="ii")
             ri = psum4.tile([P, HALF], F32, name="ri")
             product(ii, [("wi", 1, 0), ("wi", 1, 1)], n, h)
             product(rr, [("wr4", 0, 0), ("wr4", 0, 1), ("wrd", 0, 0), ("wrd", 0, 1)], n, h)
             product(ri, [("wi", 0, 0), ("wi", 0, 1), ("wr4", 1, 0), ("wrd", 1, 0), ("wr4", 1, 1), ("wrd", 1, 1)], n, h)
-            ii_sb = ring.tile([P, HALF], F32, name="ii_sb")
             nc.scalar.copy(ii_sb[:], ii[:])
             zr = ring.tile([P, HALF], F32, name="zr")
             o0 = ring.tile([P, HALF], F32, name="o0")
             o1 = ring.tile([P, HALF], F32, name="o1")
             rows, cols = slice(P * n, P * (n + 1)), slice(HALF * h, HALF * (h + 1))
+            nc.vector.tensor_tensor(zr[:], rr[:], ii_sb[:], SUB)
             nc.vector.tensor_copy(gate[:], gate_win[n][:].indirect(list_half(h)))
-            if last:
-                nc.vector.tensor_tensor(zr[:], rr[:], ii_sb[:], SUB)
-                nc.vector.tensor_tensor(o0[:], zr[:], gate[:], MULT)
-            else:
-                rr_sb = ring.tile([P, HALF], F32, name="rr_sb")
-                nc.scalar.copy(rr_sb[:], rr[:])
-                nc.gpsimd.tensor_tensor(zr[:], rr_sb[:], ii_sb[:], SUB)
-                nc.gpsimd.tensor_tensor(o0[:], zr[:], gate[:], MULT)
+            gating_engine.tensor_tensor(o0[:], zr[:], gate[:], MULT)
             nc.sync.dma_start(out_0[rows, cols], o0[:])
             nc.vector.tensor_tensor(o1[:], ri[:], gate[:], MULT)
             nc.sync.dma_start(out_1[rows, cols], o1[:])
 
-        plane0[0] = keep.tile([P, J], U8, name="plane0_0", align_bytes=64)
-        plane0[1] = keep.tile([P, J], U8, name="plane0_1", align_bytes=64)
         load_words(0)
         nc.sync.dma_start(offsets[:], offs)
         load_scales(0)
         nc.sync.dma_start(wr4_sb[:].bitcast(I32), wr4_words.rearrange("a p b -> p a b").bitcast(I32))
-        nc.sync.dma_start(wi_sb[:], wi_words.rearrange("a p n i -> p a (n i)").bitcast(I32))
+        load_words(1)
         load_weight_scales(nc.gpsimd, wi_sc, wi_scales)
         load_scales(1)
-        load_words(1)
+        nc.sync.dma_start(wi_sb[:], wi_words.rearrange("a p n i -> p a (n i)").bitcast(I32))
         load_wrd(0)
-        load_weight_scales(nc.sync, wr4_sc, wr4_scales)
         picked00 = gather_words(0, 0, picked_tile("picked00", 43008))
-        gather_scales(0, 0)
-        part_words(0, 0, picked00)
-        gather_scales(0, 1)
-        shift_scales(0)
+        gather_scales(0, 0, 32768)
+        shift_scales(nc.scalar, 0, 0)
+        load_weight_scales(nc.sync, wr4_sc, wr4_scales)
         load_wrd(1)
-        gather_scales(1, 0)
-        gather_scales(1, 1)
-        shift_scales(1)
+        part_words(0, 0, picked00)
+        picked10 = gather_words(1, 0, picked_tile("picked10", 45056))
+        gather_scales(1, 0, 33280)
+        shift_scales(nc.scalar, 1, 0)
+        part_words(1, 0, picked10)
         load_gate(0)
         load_gate(1)
-        picked10 = gather_words(1, 0, picked_tile("picked10", 45056))
-        part_words(1, 0, picked10)
+        picked01 = gather_words(0, 1, picked_tile("picked01", 45056 + 1024))
+        gather_scales(0, 1, 45056)
+        shift_scales(nc.sync, 0, 1)
+        load_gate(2)
+        part_words(0, 1, picked01)
         quantize_wrd(0, 0)
         quantize_wrd(0, 1)
-        picked01 = gather_words(0, 1, picked_tile("picked01", 45056))
-        load_gate(2)
+        gather_scales(1, 1, 34816)
+        shift_scales(nc.sync, 1, 1)
+        picked11 = gather_words(1, 1, picked_tile("picked11", 34816 + 512))
+        load_gate(3)
         quantize_wrd(1, 0)
         quantize_wrd(1, 1)
-        part_words(0, 1, picked01)
-        picked11 = gather_words(1, 1, picked_tile("picked11", 34816 + 2048 * 2))
-        load_gate(3)
         part_words(1, 1, picked11)
         order = [(n, h) for h in range(HALVES) for n in range(ROW_TILES)]
         for u, (n, h) in enumerate(order):
-            gate = staged.tile([P, HALF], F32, name="gate%d" % u, align_bytes=64, offset=57344 + 2048 * (u % 3))
-            unit(n, h, u == len(order) - 1, gate)
+            last = u == len(order) - 1
+            ii_sb = staged.tile([P, HALF], F32, name="ii_sb%d" % u, align_bytes=64, offset=57344 + 2048 * (u % 4))
+            gate = staged.tile([P, HALF], F32, name="gate%d" % u, align_bytes=64, offset=65536 if last else 57344 + 2048 * (u % 4))
+            unit(n, h, nc.vector if last else nc.gpsimd, ii_sb, gate)

@@ -49,14 +49,14 @@ def tile_list_cpxtab_dl_gate_kernel(
         wi_sb = staged.tile([P, PASSES, N], I32, name="wi_sb", align_bytes=64, offset=53248)
         plane0 = {}
         plane1 = {(v, h): keep.tile([P, HALF], U8, name="plane1_%d_%d" % (v, h), align_bytes=64) for h in range(HALVES) for v in range(2)}
-        parted = [[keep.tile([P, PASSES, 2 * HALF], U8, name="parted%d_%d" % (v, h), align_bytes=64) for h in range(HALVES)] for v in range(2)]
+        parted = {}
 
         nc.vector.memset(scale_win[0][:].bitcast(I32), 0)
         nc.vector.memset(warm[:, 0:1], 0.0)
         nc.scalar.copy(warm[:, 8:9], warm[:, 0:1])
         nc.vector.memset(scale_win[1][:].bitcast(I32), 0)
-        nc.gpsimd.memset(wi_sc[:].bitcast(I32), 0)
-        nc.vector.memset(wr4_sc[:].bitcast(I32), 0)
+        nc.gpsimd.memset(wr4_sc[:].bitcast(I32), 0)
+        nc.vector.memset(wi_sc[:].bitcast(I32), 0)
         for plane in plane1:
             nc.vector.memset(plane1[plane][:].bitcast(I32), 0)
 
@@ -65,8 +65,11 @@ def tile_list_cpxtab_dl_gate_kernel(
                 nc.sync.dma_start(scale_win[v][32 * q : 32 * q + 8, :].bitcast(I32),
                                   scales_hbm[v][:, 4 * q : 4 * q + 4, :].bitcast(I32))
 
-        def load_words(v):
-            nc.sync.dma_start(word_win[v][:], words_hbm[v][0].rearrange("p t b -> p (t b)").bitcast(I32))
+        def load_words(v, pieces):
+            words = words_hbm[v][0].rearrange("p t b -> p (t b)").bitcast(I32)
+            width = T // pieces
+            for c in range(pieces):
+                nc.sync.dma_start(word_win[v][:, width * c : width * (c + 1)], words[:, width * c : width * (c + 1)])
 
         def load_weight_scales(queue, dst, src):
             for q in range(4):
@@ -100,8 +103,9 @@ def tile_list_cpxtab_dl_gate_kernel(
             nc.vector.tensor_copy(picked[:], word_win[v][:].bitcast(U32).indirect(list_half(h)))
             return picked
 
-        def part_words(v, h, picked):
-            nc.vector.tensor_copy(parted[v][h][:].bitcast(U16), picked[:].bitcast(U16).rearrange("p (j a) -> p a j", a=PASSES))
+        def part_words(v, h, picked, offset):
+            parted[v, h] = staged.tile([P, PASSES, 2 * HALF], U8, name="parted%d_%d" % (v, h), align_bytes=64, offset=offset)
+            nc.vector.tensor_copy(parted[v, h][:].bitcast(U16), picked[:].bitcast(U16).rearrange("p (j a) -> p a j", a=PASSES))
 
         def picked_tile(name, offset):
             return staged.tile([P, HALF], U32, name=name, align_bytes=64, offset=offset)
@@ -132,12 +136,12 @@ def tile_list_cpxtab_dl_gate_kernel(
                 w, w_sc = weight(name, n, a)
                 nc.tensor.matmul_mx(
                     out=acc[:], lhsT=w, lhsT_scale=w_sc,
-                    rhs=parted[v][h][:, a, :].bitcast(FP4X4),
+                    rhs=parted[v, h][:, a, :].bitcast(FP4X4),
                     rhs_scale=(plane0, plane1)[a][v, h][:],
                     start=(s == 0), stop=(s == len(steps) - 1),
                 )
 
-        def unit(n, h, gating_engine, ii_sb, gate):
+        def unit(n, h, offload_difference, gating_engine, ii_sb, gate):
             rr = psum2.tile([P, HALF], F32, name="rr")
             ii = psum2.tile([P, HALF], F32, name="ii")
             ri = psum4.tile([P, HALF], F32, name="ri")
@@ -149,51 +153,57 @@ def tile_list_cpxtab_dl_gate_kernel(
             o0 = ring.tile([P, HALF], F32, name="o0")
             o1 = ring.tile([P, HALF], F32, name="o1")
             rows, cols = slice(P * n, P * (n + 1)), slice(HALF * h, HALF * (h + 1))
-            nc.vector.tensor_tensor(zr[:], rr[:], ii_sb[:], SUB)
+            if offload_difference:
+                rr_sb = ring.tile([P, HALF], F32, name="rr_sb")
+                nc.scalar.copy(rr_sb[:], rr[:])
+                nc.gpsimd.tensor_tensor(zr[:], rr_sb[:], ii_sb[:], SUB)
+            else:
+                nc.vector.tensor_tensor(zr[:], rr[:], ii_sb[:], SUB)
             nc.vector.tensor_copy(gate[:], gate_win[n][:].indirect(list_half(h)))
             gating_engine.tensor_tensor(o0[:], zr[:], gate[:], MULT)
             nc.sync.dma_start(out_0[rows, cols], o0[:])
             nc.vector.tensor_tensor(o1[:], ri[:], gate[:], MULT)
             nc.sync.dma_start(out_1[rows, cols], o1[:])
 
-        load_words(0)
         nc.sync.dma_start(offsets[:], offs)
+        load_words(0, 4)
         load_scales(0)
         nc.sync.dma_start(wr4_sb[:].bitcast(I32), wr4_words.rearrange("a p b -> p a b").bitcast(I32))
-        load_words(1)
-        load_weight_scales(nc.gpsimd, wi_sc, wi_scales)
+        load_weight_scales(nc.gpsimd, wr4_sc, wr4_scales)
+        load_words(1, 1)
         load_scales(1)
         nc.sync.dma_start(wi_sb[:], wi_words.rearrange("a p n i -> p a (n i)").bitcast(I32))
-        load_wrd(0)
+        load_weight_scales(nc.sync, wi_sc, wi_scales)
         picked00 = gather_words(0, 0, picked_tile("picked00", 43008))
         gather_scales(0, 0, 32768)
-        shift_scales(nc.scalar, 0, 0)
-        load_weight_scales(nc.sync, wr4_sc, wr4_scales)
-        load_wrd(1)
-        part_words(0, 0, picked00)
+        shift_scales(nc.sync, 0, 0)
+        load_wrd(0)
+        part_words(0, 0, picked00, 67584)
         picked10 = gather_words(1, 0, picked_tile("picked10", 45056))
         gather_scales(1, 0, 33280)
-        shift_scales(nc.scalar, 1, 0)
-        part_words(1, 0, picked10)
+        shift_scales(nc.sync, 1, 0)
+        load_wrd(1)
         load_gate(0)
-        load_gate(1)
+        part_words(1, 0, picked10, 69632)
         picked01 = gather_words(0, 1, picked_tile("picked01", 45056 + 1024))
         gather_scales(0, 1, 45056)
         shift_scales(nc.sync, 0, 1)
+        load_gate(1)
         load_gate(2)
-        part_words(0, 1, picked01)
         quantize_wrd(0, 0)
+        part_words(0, 1, picked01, 34816)
         quantize_wrd(0, 1)
-        gather_scales(1, 1, 34816)
+        gather_scales(1, 1, 36864)
         shift_scales(nc.sync, 1, 1)
-        picked11 = gather_words(1, 1, picked_tile("picked11", 34816 + 512))
-        load_gate(3)
         quantize_wrd(1, 0)
         quantize_wrd(1, 1)
-        part_words(1, 1, picked11)
+        picked11 = gather_words(1, 1, picked_tile("picked11", 40960))
+        load_gate(3)
+        part_words(1, 1, picked11, 71680)
         order = [(n, h) for h in range(HALVES) for n in range(ROW_TILES)]
         for u, (n, h) in enumerate(order):
             last = u == len(order) - 1
-            ii_sb = staged.tile([P, HALF], F32, name="ii_sb%d" % u, align_bytes=64, offset=57344 + 2048 * (u % 4))
-            gate = staged.tile([P, HALF], F32, name="gate%d" % u, align_bytes=64, offset=65536 if last else 57344 + 2048 * (u % 4))
-            unit(n, h, nc.vector if last else nc.gpsimd, ii_sb, gate)
+            ii_sb = staged.tile([P, HALF], F32, name="ii_sb%d" % u, align_bytes=64, offset=57344 + 2048 * n)
+            held = h == 1 and not last
+            gate = staged.tile([P, HALF], F32, name="gate%d" % u, align_bytes=64, offset=(57344 if held else 73728) + 2048 * n)
+            unit(n, h, h == 0, nc.vector if last else nc.gpsimd, ii_sb, gate)

@@ -17,11 +17,34 @@ MULT = mybir.AluOpType.mult
 SUB = mybir.AluOpType.subtract
 
 P = 128
-PASSES = 2
+PACK = 4
+K_PASS = P * PACK
+PASSES = K // K_PASS
+QUADRANTS = 4
 HALF = 512
 HALVES = J // HALF
 ROW_TILES = N // P
-LIST_COLS = HALF // 16
+PAIR = 2 * P
+REAL, IMAG = 0, 1
+ALIGN = 64
+
+MOVED_ROWS = 112
+FIRST_TABLE_PIECES = 4
+
+WINDOW = 4 * T
+SLOT = 4 * HALF
+WORDS_AT = 0
+REAL_SCALES_AT = WORDS_AT + 2 * WINDOW
+FIRST_PLANES_AT = REAL_SCALES_AT + SLOT
+GROUPED_AT = FIRST_PLANES_AT + SLOT
+PICKED_REAL_AT = GROUPED_AT + 4 * SLOT
+II_AT = PICKED_REAL_AT + SLOT
+SECOND_GATE_ROWS_AT = II_AT + ROW_TILES * SLOT
+SECOND_REAL_PLANE_AT = SECOND_GATE_ROWS_AT + WINDOW
+FIRST_GATE_ROWS_AT = SECOND_REAL_PLANE_AT + HALF
+GATES_AT = FIRST_GATE_ROWS_AT + WINDOW
+PICKED_IMAG_AT = SECOND_REAL_PLANE_AT - ALIGN
+GATE_ROWS_AT = (FIRST_GATE_ROWS_AT, SECOND_GATE_ROWS_AT, WORDS_AT, WORDS_AT + WINDOW)
 
 
 def tile_list_cpxtab_dl_gate_kernel(
@@ -31,179 +54,178 @@ def tile_list_cpxtab_dl_gate_kernel(
     nc = tc.nc
     with ExitStack() as ctx:
         keep = ctx.enter_context(tc.tile_pool(name="keep", bufs=1))
-        ring = ctx.enter_context(tc.tile_pool(name="ring", bufs=4))
-        psum4 = ctx.enter_context(tc.psum_pool(name="psum4", bufs=4))
-        psum2 = ctx.enter_context(tc.psum_pool(name="psum2", bufs=2))
+        placed = ctx.enter_context(tc.tile_pool(name="placed", bufs=1))
+        ring = ctx.enter_context(tc.tile_pool(name="ring", bufs=ROW_TILES))
+        psum_ri = ctx.enter_context(tc.psum_pool(name="psum_ri", bufs=4))
+        psum_rr_ii = ctx.enter_context(tc.psum_pool(name="psum_rr_ii", bufs=2))
 
-        staged = ctx.enter_context(tc.tile_pool(name="staged", bufs=1))
+        def place(shape, dtype, name, offset):
+            return placed.tile(shape, dtype, name=name, align_bytes=ALIGN, offset=offset)
+
+        def hold(shape, dtype, name):
+            return keep.tile(shape, dtype, name=name, align_bytes=ALIGN)
+
         offsets = keep.tile([P, J // 16], U16, name="offsets")
-
         words_hbm = (tab_words, tab2_words)
         scales_hbm = (tab_scales, tab2_scales)
-        warm = keep.tile([P, 16], F32, name="warm")
-        word_win = [staged.tile([P, T], I32, name="word_win%d" % v, align_bytes=64, offset=(16384, 24576)[v]) for v in range(2)]
-        scale_win = [keep.tile([P, T], U8, name="scale_win%d" % v, align_bytes=64) for v in range(2)]
-        wr4_sc = keep.tile([P, PASSES, N], U8, name="wr4_sc", align_bytes=64)
-        wi_sc = keep.tile([P, PASSES, N], U8, name="wi_sc", align_bytes=64)
-        wr4_sb = staged.tile([P, PASSES, 2 * N], U8, name="wr4_sb", align_bytes=64, offset=51200)
-        wi_sb = staged.tile([P, PASSES, N], I32, name="wi_sb", align_bytes=64, offset=53248)
-        plane0 = {}
-        plane1 = {(v, h): keep.tile([P, HALF], U8, name="plane1_%d_%d" % (v, h), align_bytes=64) for h in range(HALVES) for v in range(2)}
-        parted = {}
+        word_win = [place([P, T], I32, "word_win%d" % v, WORDS_AT + WINDOW * v) for v in (REAL, IMAG)]
+        scale_win = [place([P, T], U8, "scale_win_real", REAL_SCALES_AT), hold([P, T], U8, "scale_win_imag")]
+        wr4_sb = hold([P, PASSES, 2 * N], U8, "wr4_sb")
+        wr4_sc = hold([P, PASSES, N], U8, "wr4_sc")
+        wi_sb = hold([P, PASSES, N], I32, "wi_sb")
+        wi_sc = hold([P, PASSES, N], U8, "wi_sc")
+        plane_pass1 = {(v, h): hold([P, HALF], U8, "plane_pass1_%d_%d" % (v, h))
+                       for h in range(HALVES) for v in (REAL, IMAG)}
+        plane_pass0, parted, wrd_raw, wrd_codes, wrd_sc, gate_win = {}, {}, {}, {}, {}, {}
 
-        nc.vector.memset(scale_win[0][:].bitcast(I32), 0)
-        nc.vector.memset(warm[:, 0:1], 0.0)
-        nc.scalar.copy(warm[:, 8:9], warm[:, 0:1])
-        nc.vector.memset(scale_win[1][:].bitcast(I32), 0)
+        nc.vector.memset(scale_win[REAL][:].bitcast(I32), 0)
+        nc.vector.memset(scale_win[IMAG][:].bitcast(I32), 0)
         nc.gpsimd.memset(wr4_sc[:].bitcast(I32), 0)
         nc.vector.memset(wi_sc[:].bitcast(I32), 0)
-        for plane in plane1:
-            nc.vector.memset(plane1[plane][:].bitcast(I32), 0)
-
-        def load_scales(v):
-            for q in range(4):
-                nc.sync.dma_start(scale_win[v][32 * q : 32 * q + 8, :].bitcast(I32),
-                                  scales_hbm[v][:, 4 * q : 4 * q + 4, :].bitcast(I32))
+        for key in plane_pass1:
+            nc.vector.memset(plane_pass1[key][:].bitcast(I32), 0)
 
         def load_words(v, pieces):
             words = words_hbm[v][0].rearrange("p t b -> p (t b)").bitcast(I32)
             width = T // pieces
             for c in range(pieces):
-                nc.sync.dma_start(word_win[v][:, width * c : width * (c + 1)], words[:, width * c : width * (c + 1)])
+                cols = slice(width * c, width * (c + 1))
+                nc.sync.dma_start(word_win[v][:, cols], words[:, cols])
 
-        def load_weight_scales(queue, dst, src):
-            for q in range(4):
-                queue.dma_start(dst[32 * q : 32 * q + 4, :, :].bitcast(I32),
-                                    src[:, 4 * q : 4 * q + 4, :].rearrange("a r n -> r a n").bitcast(I32))
+        def load_table_scales(v):
+            for q in range(QUADRANTS):
+                nc.sync.dma_start(scale_win[v][32 * q : 32 * q + 4 * PASSES, :].bitcast(I32),
+                                  scales_hbm[v][:, 4 * q : 4 * q + 4, :].bitcast(I32))
 
-        wrd_raw = {}
-        gate_win = {}
+        def load_weight_scales(queue, planes, scales):
+            for q in range(QUADRANTS):
+                queue.dma_start(planes[32 * q : 32 * q + 4, :, :].bitcast(I32),
+                                scales[:, 4 * q : 4 * q + 4, :].rearrange("a r n -> r a n").bitcast(I32))
 
-        def load_wrd(a):
-            raw = keep.tile([P, 4, N], F32, name="wrd_raw%d" % a)
-            nc.sync.dma_start(raw[:], wrd[512 * a : 512 * (a + 1), :].rearrange("(p i) n -> p i n", i=4))
+        def load_wrd(a, raw):
+            rows = wrd[K_PASS * a : K_PASS * (a + 1), :]
+            nc.sync.dma_start(raw[:], rows.rearrange("(p i) n -> p i n", i=PACK))
             wrd_raw[a] = raw
 
-        def load_gate(n):
-            win = staged.tile([P, T], F32, name="gate_win%d" % n, align_bytes=64, offset=8192 * n)
-            nc.sync.dma_start(win[:], gT[P * n : P * (n + 1), :])
-            gate_win[n] = win
+        def load_gate_rows(n):
+            gate_win[n] = place([P, T], F32, "gate_win%d" % n, GATE_ROWS_AT[n])
+            nc.sync.dma_start(gate_win[n][:], gT[P * n : P * (n + 1), :])
 
         def list_half(h):
-            return offsets[:, LIST_COLS * h : LIST_COLS * (h + 1)]
+            return offsets[:, HALF // 16 * h : HALF // 16 * (h + 1)]
 
         def gather_scales(v, h, offset):
-            plane0[v, h] = staged.tile([P, HALF], U8, name="plane0_%d_%d" % (v, h), align_bytes=64, offset=offset)
-            nc.vector.tensor_copy(plane0[v, h][:], scale_win[v][:].indirect(list_half(h)))
+            plane_pass0[v, h] = place([P, HALF], U8, "plane_pass0_%d_%d" % (v, h), offset)
+            nc.vector.tensor_copy(plane_pass0[v, h][:], scale_win[v][:].indirect(list_half(h)))
+            nc.sync.dma_start(plane_pass1[v, h][0:MOVED_ROWS, :].bitcast(I32),
+                              plane_pass0[v, h][4 : 4 + MOVED_ROWS, :].bitcast(I32))
 
-        def shift_scales(queue, v, h):
-            queue.dma_start(plane1[v, h][0:112, :].bitcast(I32), plane0[v, h][4:116, :].bitcast(I32))
-
-        def gather_words(v, h, picked):
+        def gather_words(v, h, offset):
+            picked = place([P, HALF], U32, "picked%d_%d" % (v, h), offset)
             nc.vector.tensor_copy(picked[:], word_win[v][:].bitcast(U32).indirect(list_half(h)))
             return picked
 
-        def part_words(v, h, picked, offset):
-            parted[v, h] = staged.tile([P, PASSES, 2 * HALF], U8, name="parted%d_%d" % (v, h), align_bytes=64, offset=offset)
-            nc.vector.tensor_copy(parted[v, h][:].bitcast(U16), picked[:].bitcast(U16).rearrange("p (j a) -> p a j", a=PASSES))
+        def part_words(v, h, picked, target):
+            parted[v, h] = target
+            nc.vector.tensor_copy(target[:].bitcast(U16),
+                                  picked[:].bitcast(U16).rearrange("p (j a) -> p a j", a=PASSES))
 
-        def picked_tile(name, offset):
-            return staged.tile([P, HALF], U32, name=name, align_bytes=64, offset=offset)
-
-        wrd_codes = {}
-        wrd_sc = {}
+        def grouped_at(a, pair):
+            return GROUPED_AT + SLOT * (2 * a + pair)
 
         def quantize_wrd(a, pair):
-            grouped = staged.tile([P, 2 * P, 4], BF16, name="grouped%d_%d" % (a, pair), align_bytes=64, offset=34816 + 2048 * (2 * a + pair))
-            src = wrd_raw[a][:, :, 2 * P * pair : 2 * P * (pair + 1)]
-            nc.scalar.copy(grouped[:].rearrange("p (c x) i -> p c i x", x=4), src.rearrange("p i (c x) -> p c i x", x=4))
-            codes = keep.tile([P, 2 * P], U32, name="wrd_codes%d_%d" % (a, pair), align_bytes=64)
-            sc = keep.tile([P, 2 * P], U8, name="wrd_sc%d_%d" % (a, pair), align_bytes=64)
-            nc.vector.quantize_mx(out=codes[:].bitcast(FP8X4), scales=sc[:], in_=grouped[:].rearrange("p c i -> p (c i)"))
-            wrd_codes[a, pair] = codes
-            wrd_sc[a, pair] = sc
+            grouped = place([P, PAIR, PACK], BF16, "grouped%d_%d" % (a, pair), grouped_at(a, pair))
+            rows = wrd_raw[a][:, :, PAIR * pair : PAIR * (pair + 1)]
+            nc.scalar.copy(grouped[:].rearrange("p (c x) i -> p c i x", x=4),
+                           rows.rearrange("p i (c x) -> p c i x", x=4))
+            wrd_codes[a, pair] = hold([P, PAIR], U32, "wrd_codes%d_%d" % (a, pair))
+            wrd_sc[a, pair] = hold([P, PAIR], U8, "wrd_sc%d_%d" % (a, pair))
+            nc.vector.quantize_mx(out=wrd_codes[a, pair][:].bitcast(FP8X4), scales=wrd_sc[a, pair][:],
+                                  in_=grouped[:].rearrange("p c i -> p (c i)"))
 
         def weight(name, n, a):
+            cols = slice(P * n, P * (n + 1))
             if name == "wr4":
-                return wr4_sb[:, a, 2 * P * n : 2 * P * (n + 1)].bitcast(FP4X4), wr4_sc[:, a, P * n : P * (n + 1)]
+                return wr4_sb[:, a, 2 * P * n : 2 * P * (n + 1)].bitcast(FP4X4), wr4_sc[:, a, cols]
             if name == "wi":
-                return wi_sb[:, a, P * n : P * (n + 1)].bitcast(FP8X4), wi_sc[:, a, P * n : P * (n + 1)]
-            cols = slice(P * (n % 2), P * (n % 2 + 1))
-            return wrd_codes[a, n // 2][:, cols].bitcast(FP8X4), wrd_sc[a, n // 2][:, cols]
+                return wi_sb[:, a, cols].bitcast(FP8X4), wi_sc[:, a, cols]
+            in_pair = slice(P * (n % 2), P * (n % 2 + 1))
+            return wrd_codes[a, n // 2][:, in_pair].bitcast(FP8X4), wrd_sc[a, n // 2][:, in_pair]
 
         def product(acc, steps, n, h):
             for s, (name, v, a) in enumerate(steps):
-                w, w_sc = weight(name, n, a)
+                codes, scales = weight(name, n, a)
                 nc.tensor.matmul_mx(
-                    out=acc[:], lhsT=w, lhsT_scale=w_sc,
+                    out=acc[:], lhsT=codes, lhsT_scale=scales,
                     rhs=parted[v, h][:, a, :].bitcast(FP4X4),
-                    rhs_scale=(plane0, plane1)[a][v, h][:],
+                    rhs_scale=(plane_pass0, plane_pass1)[a][v, h][:],
                     start=(s == 0), stop=(s == len(steps) - 1),
                 )
 
-        def unit(n, h, offload_difference, gating_engine, ii_sb, gate):
-            rr = psum2.tile([P, HALF], F32, name="rr")
-            ii = psum2.tile([P, HALF], F32, name="ii")
-            ri = psum4.tile([P, HALF], F32, name="ri")
-            product(ii, [("wi", 1, 0), ("wi", 1, 1)], n, h)
-            product(rr, [("wr4", 0, 0), ("wr4", 0, 1), ("wrd", 0, 0), ("wrd", 0, 1)], n, h)
-            product(ri, [("wi", 0, 0), ("wi", 0, 1), ("wr4", 1, 0), ("wrd", 1, 0), ("wr4", 1, 1), ("wrd", 1, 1)], n, h)
+        def output_tile(n, h, gate_at):
+            last = n == ROW_TILES - 1 and h == HALVES - 1
+            rr = psum_rr_ii.tile([P, HALF], F32, name="rr")
+            ii = psum_rr_ii.tile([P, HALF], F32, name="ii")
+            ri = psum_ri.tile([P, HALF], F32, name="ri")
+            product(ii, [("wi", IMAG, 0), ("wi", IMAG, 1)], n, h)
+            product(rr, [("wr4", REAL, 0), ("wr4", REAL, 1), ("wrd", REAL, 0), ("wrd", REAL, 1)], n, h)
+            product(ri, [("wi", REAL, 0), ("wi", REAL, 1), ("wr4", IMAG, 0), ("wrd", IMAG, 0),
+                         ("wr4", IMAG, 1), ("wrd", IMAG, 1)], n, h)
+            ii_sb = place([P, HALF], F32, "ii_sb%d_%d" % (n, h), II_AT + SLOT * n)
             nc.scalar.copy(ii_sb[:], ii[:])
             zr = ring.tile([P, HALF], F32, name="zr")
-            o0 = ring.tile([P, HALF], F32, name="o0")
-            o1 = ring.tile([P, HALF], F32, name="o1")
-            rows, cols = slice(P * n, P * (n + 1)), slice(HALF * h, HALF * (h + 1))
-            if offload_difference:
+            result_0 = ring.tile([P, HALF], F32, name="result_0")
+            result_1 = ring.tile([P, HALF], F32, name="result_1")
+            if h == 0:
                 rr_sb = ring.tile([P, HALF], F32, name="rr_sb")
                 nc.scalar.copy(rr_sb[:], rr[:])
                 nc.gpsimd.tensor_tensor(zr[:], rr_sb[:], ii_sb[:], SUB)
             else:
                 nc.vector.tensor_tensor(zr[:], rr[:], ii_sb[:], SUB)
+            gate = place([P, HALF], F32, "gate%d_%d" % (n, h), gate_at)
             nc.vector.tensor_copy(gate[:], gate_win[n][:].indirect(list_half(h)))
-            gating_engine.tensor_tensor(o0[:], zr[:], gate[:], MULT)
-            nc.sync.dma_start(out_0[rows, cols], o0[:])
-            nc.vector.tensor_tensor(o1[:], ri[:], gate[:], MULT)
-            nc.sync.dma_start(out_1[rows, cols], o1[:])
+            rows, cols = slice(P * n, P * (n + 1)), slice(HALF * h, HALF * (h + 1))
+            (nc.vector if last else nc.gpsimd).tensor_tensor(result_0[:], zr[:], gate[:], MULT)
+            nc.sync.dma_start(out_0[rows, cols], result_0[:])
+            nc.vector.tensor_tensor(result_1[:], ri[:], gate[:], MULT)
+            nc.sync.dma_start(out_1[rows, cols], result_1[:])
 
         nc.sync.dma_start(offsets[:], offs)
-        load_words(0, 4)
-        load_scales(0)
+        load_words(REAL, FIRST_TABLE_PIECES)
+        load_table_scales(REAL)
         nc.sync.dma_start(wr4_sb[:].bitcast(I32), wr4_words.rearrange("a p b -> p a b").bitcast(I32))
         load_weight_scales(nc.gpsimd, wr4_sc, wr4_scales)
-        load_words(1, 1)
-        load_scales(1)
         nc.sync.dma_start(wi_sb[:], wi_words.rearrange("a p n i -> p a (n i)").bitcast(I32))
+        load_table_scales(IMAG)
+        load_words(IMAG, 1)
         load_weight_scales(nc.sync, wi_sc, wi_scales)
-        picked00 = gather_words(0, 0, picked_tile("picked00", 43008))
-        gather_scales(0, 0, 32768)
-        shift_scales(nc.sync, 0, 0)
-        load_wrd(0)
-        part_words(0, 0, picked00, 67584)
-        picked10 = gather_words(1, 0, picked_tile("picked10", 45056))
-        gather_scales(1, 0, 33280)
-        shift_scales(nc.sync, 1, 0)
-        load_wrd(1)
-        load_gate(0)
-        part_words(1, 0, picked10, 69632)
-        picked01 = gather_words(0, 1, picked_tile("picked01", 45056 + 1024))
-        gather_scales(0, 1, 45056)
-        shift_scales(nc.sync, 0, 1)
-        load_gate(1)
-        load_gate(2)
+
+        parted_shape = [P, PASSES, 2 * HALF]
+        picked_real = gather_words(REAL, 0, PICKED_REAL_AT)
+        gather_scales(REAL, 0, FIRST_PLANES_AT)
+        load_wrd(0, hold([P, PACK, N], F32, "wrd_raw0"))
+        part_words(REAL, 0, picked_real, hold(parted_shape, U8, "parted_real0"))
+        gather_scales(IMAG, 0, FIRST_PLANES_AT + HALF)
+        load_wrd(1, place([P, PACK, N], F32, "wrd_raw1", II_AT))
+        picked_imag = gather_words(IMAG, 0, PICKED_IMAG_AT)
+        part_words(IMAG, 0, picked_imag, hold(parted_shape, U8, "parted_imag0"))
+        load_gate_rows(0)
+        load_gate_rows(1)
+
+        gather_scales(REAL, 1, SECOND_REAL_PLANE_AT)
+        picked_real = gather_words(REAL, 1, REAL_SCALES_AT)
+        load_gate_rows(2)
         quantize_wrd(0, 0)
-        part_words(0, 1, picked01, 34816)
+        part_words(REAL, 1, picked_real, place(parted_shape, U8, "parted_real1", grouped_at(0, 0)))
         quantize_wrd(0, 1)
-        gather_scales(1, 1, 36864)
-        shift_scales(nc.sync, 1, 1)
+        gather_scales(IMAG, 1, grouped_at(0, 1))
         quantize_wrd(1, 0)
         quantize_wrd(1, 1)
-        picked11 = gather_words(1, 1, picked_tile("picked11", 40960))
-        load_gate(3)
-        part_words(1, 1, picked11, 71680)
-        order = [(n, h) for h in range(HALVES) for n in range(ROW_TILES)]
-        for u, (n, h) in enumerate(order):
-            last = u == len(order) - 1
-            ii_sb = staged.tile([P, HALF], F32, name="ii_sb%d" % u, align_bytes=64, offset=57344 + 2048 * n)
-            held = h == 1 and not last
-            gate = staged.tile([P, HALF], F32, name="gate%d" % u, align_bytes=64, offset=(57344 if held else 73728) + 2048 * n)
-            unit(n, h, h == 0, nc.vector if last else nc.gpsimd, ii_sb, gate)
+        picked_imag = gather_words(IMAG, 1, grouped_at(1, 1) + SLOT // 2)
+        load_gate_rows(3)
+        part_words(IMAG, 1, picked_imag, hold(parted_shape, U8, "parted_imag1"))
+
+        for n in range(ROW_TILES):
+            output_tile(n, 0, grouped_at(1, 1) - SLOT // 2 if n == 0 else GATES_AT + SLOT * n)
+        for n in range(ROW_TILES):
+            output_tile(n, 1, GATES_AT if n == ROW_TILES - 1 else II_AT + SLOT * n)

from contextlib import ExitStack

import concourse.mybir as mybir

K, N, T, J = 1024, 512, 2048, 1024
FLOPS = 6 * 2 * K * N * J

F32 = mybir.dt.float32
BF16 = mybir.dt.bfloat16
I32 = mybir.dt.int32
U32 = mybir.dt.uint32
U16 = mybir.dt.uint16
U8 = mybir.dt.uint8
FP8X4 = mybir.dt.float8_e4m3fn_x4
FP4X4 = mybir.dt.float4_e2m1fn_x4
MULT = mybir.AluOpType.mult
SUB = mybir.AluOpType.subtract

P = 128
PACK = 4
K_PASS = P * PACK
PASSES = K // K_PASS
QUADRANTS = 4
HALF = 512
HALVES = J // HALF
ROW_TILES = N // P
PAIR = 2 * P
REAL, IMAG = 0, 1
ALIGN = 64

MOVED_ROWS = 112
FIRST_TABLE_PIECES = 4

WINDOW = 4 * T
SLOT = 4 * HALF
WORDS_AT = 0
REAL_SCALES_AT = WORDS_AT + 2 * WINDOW
FIRST_PLANES_AT = REAL_SCALES_AT + SLOT
GROUPED_AT = FIRST_PLANES_AT + SLOT
PICKED_REAL_AT = GROUPED_AT + 4 * SLOT
II_AT = PICKED_REAL_AT + SLOT
SECOND_GATE_ROWS_AT = II_AT + ROW_TILES * SLOT
SECOND_REAL_PLANE_AT = SECOND_GATE_ROWS_AT + WINDOW
FIRST_GATE_ROWS_AT = SECOND_REAL_PLANE_AT + HALF
GATES_AT = FIRST_GATE_ROWS_AT + WINDOW
PICKED_IMAG_AT = SECOND_REAL_PLANE_AT - ALIGN
GATE_ROWS_AT = (FIRST_GATE_ROWS_AT, SECOND_GATE_ROWS_AT, WORDS_AT, WORDS_AT + WINDOW)


def tile_list_cpxtab_dl_gate_kernel(
    tc, tab_words, tab_scales, tab2_words, tab2_scales, wr4_words, wr4_scales,
    wrd, wi_words, wi_scales, gT, offs, out_0, out_1,
):
    nc = tc.nc
    with ExitStack() as ctx:
        keep = ctx.enter_context(tc.tile_pool(name="keep", bufs=1))
        placed = ctx.enter_context(tc.tile_pool(name="placed", bufs=1))
        ring = ctx.enter_context(tc.tile_pool(name="ring", bufs=ROW_TILES))
        psum_ri = ctx.enter_context(tc.psum_pool(name="psum_ri", bufs=4))
        psum_rr_ii = ctx.enter_context(tc.psum_pool(name="psum_rr_ii", bufs=2))

        def place(shape, dtype, name, offset):
            return placed.tile(shape, dtype, name=name, align_bytes=ALIGN, offset=offset)

        def hold(shape, dtype, name):
            return keep.tile(shape, dtype, name=name, align_bytes=ALIGN)

        offsets = keep.tile([P, J // 16], U16, name="offsets")
        words_hbm = (tab_words, tab2_words)
        scales_hbm = (tab_scales, tab2_scales)
        word_win = [place([P, T], I32, "word_win%d" % v, WORDS_AT + WINDOW * v) for v in (REAL, IMAG)]
        scale_win = [place([P, T], U8, "scale_win_real", REAL_SCALES_AT), hold([P, T], U8, "scale_win_imag")]
        wr4_sb = hold([P, PASSES, 2 * N], U8, "wr4_sb")
        wr4_sc = hold([P, PASSES, N], U8, "wr4_sc")
        wi_sb = hold([P, PASSES, N], I32, "wi_sb")
        wi_sc = hold([P, PASSES, N], U8, "wi_sc")
        plane_pass1 = {(v, h): hold([P, HALF], U8, "plane_pass1_%d_%d" % (v, h))
                       for h in range(HALVES) for v in (REAL, IMAG)}
        plane_pass0, parted, wrd_raw, wrd_codes, wrd_sc, gate_win = {}, {}, {}, {}, {}, {}

        nc.vector.memset(scale_win[REAL][:].bitcast(I32), 0)
        nc.vector.memset(scale_win[IMAG][:].bitcast(I32), 0)
        nc.gpsimd.memset(wr4_sc[:].bitcast(I32), 0)
        nc.vector.memset(wi_sc[:].bitcast(I32), 0)
        for key in plane_pass1:
            nc.vector.memset(plane_pass1[key][:].bitcast(I32), 0)

        def load_words(v, pieces):
            words = words_hbm[v][0].rearrange("p t b -> p (t b)").bitcast(I32)
            width = T // pieces
            for c in range(pieces):
                cols = slice(width * c, width * (c + 1))
                nc.sync.dma_start(word_win[v][:, cols], words[:, cols])

        def load_table_scales(v):
            for q in range(QUADRANTS):
                nc.sync.dma_start(scale_win[v][32 * q : 32 * q + 4 * PASSES, :].bitcast(I32),
                                  scales_hbm[v][:, 4 * q : 4 * q + 4, :].bitcast(I32))

        def load_weight_scales(queue, planes, scales):
            for q in range(QUADRANTS):
                queue.dma_start(planes[32 * q : 32 * q + 4, :, :].bitcast(I32),
                                scales[:, 4 * q : 4 * q + 4, :].rearrange("a r n -> r a n").bitcast(I32))

        def load_wrd(a, raw):
            rows = wrd[K_PASS * a : K_PASS * (a + 1), :]
            nc.sync.dma_start(raw[:], rows.rearrange("(p i) n -> p i n", i=PACK))
            wrd_raw[a] = raw

        def load_gate_rows(n):
            gate_win[n] = place([P, T], F32, "gate_win%d" % n, GATE_ROWS_AT[n])
            nc.sync.dma_start(gate_win[n][:], gT[P * n : P * (n + 1), :])

        def list_half(h):
            return offsets[:, HALF // 16 * h : HALF // 16 * (h + 1)]

        def gather_scales(v, h, offset):
            plane_pass0[v, h] = place([P, HALF], U8, "plane_pass0_%d_%d" % (v, h), offset)
            nc.vector.tensor_copy(plane_pass0[v, h][:], scale_win[v][:].indirect(list_half(h)))
            nc.sync.dma_start(plane_pass1[v, h][0:MOVED_ROWS, :].bitcast(I32),
                              plane_pass0[v, h][4 : 4 + MOVED_ROWS, :].bitcast(I32))

        def gather_words(v, h, offset):
            picked = place([P, HALF], U32, "picked%d_%d" % (v, h), offset)
            nc.vector.tensor_copy(picked[:], word_win[v][:].bitcast(U32).indirect(list_half(h)))
            return picked

        def part_words(v, h, picked, target):
            parted[v, h] = target
            nc.vector.tensor_copy(target[:].bitcast(U16),
                                  picked[:].bitcast(U16).rearrange("p (j a) -> p a j", a=PASSES))

        def grouped_at(a, pair):
            return GROUPED_AT + SLOT * (2 * a + pair)

        def quantize_wrd(a, pair):
            grouped = place([P, PAIR, PACK], BF16, "grouped%d_%d" % (a, pair), grouped_at(a, pair))
            rows = wrd_raw[a][:, :, PAIR * pair : PAIR * (pair + 1)]
            nc.scalar.copy(grouped[:].rearrange("p (c x) i -> p c i x", x=4),
                           rows.rearrange("p i (c x) -> p c i x", x=4))
            wrd_codes[a, pair] = hold([P, PAIR], U32, "wrd_codes%d_%d" % (a, pair))
            wrd_sc[a, pair] = hold([P, PAIR], U8, "wrd_sc%d_%d" % (a, pair))
            nc.vector.quantize_mx(out=wrd_codes[a, pair][:].bitcast(FP8X4), scales=wrd_sc[a, pair][:],
                                  in_=grouped[:].rearrange("p c i -> p (c i)"))

        def weight(name, n, a):
            cols = slice(P * n, P * (n + 1))
            if name == "wr4":
                return wr4_sb[:, a, 2 * P * n : 2 * P * (n + 1)].bitcast(FP4X4), wr4_sc[:, a, cols]
            if name == "wi":
                return wi_sb[:, a, cols].bitcast(FP8X4), wi_sc[:, a, cols]
            in_pair = slice(P * (n % 2), P * (n % 2 + 1))
            return wrd_codes[a, n // 2][:, in_pair].bitcast(FP8X4), wrd_sc[a, n // 2][:, in_pair]

        def product(acc, steps, n, h):
            for s, (name, v, a) in enumerate(steps):
                codes, scales = weight(name, n, a)
                nc.tensor.matmul_mx(
                    out=acc[:], lhsT=codes, lhsT_scale=scales,
                    rhs=parted[v, h][:, a, :].bitcast(FP4X4),
                    rhs_scale=(plane_pass0, plane_pass1)[a][v, h][:],
                    start=(s == 0), stop=(s == len(steps) - 1),
                )

        def output_tile(n, h, gate_at):
            last = n == ROW_TILES - 1 and h == HALVES - 1
            rr = psum_rr_ii.tile([P, HALF], F32, name="rr")
            ii = psum_rr_ii.tile([P, HALF], F32, name="ii")
            ri = psum_ri.tile([P, HALF], F32, name="ri")
            product(ii, [("wi", IMAG, 0), ("wi", IMAG, 1)], n, h)
            product(rr, [("wr4", REAL, 0), ("wr4", REAL, 1), ("wrd", REAL, 0), ("wrd", REAL, 1)], n, h)
            product(ri, [("wi", REAL, 0), ("wi", REAL, 1), ("wr4", IMAG, 0), ("wrd", IMAG, 0),
                         ("wr4", IMAG, 1), ("wrd", IMAG, 1)], n, h)
            ii_sb = place([P, HALF], F32, "ii_sb%d_%d" % (n, h), II_AT + SLOT * n)
            nc.scalar.copy(ii_sb[:], ii[:])
            zr = ring.tile([P, HALF], F32, name="zr")
            result_0 = ring.tile([P, HALF], F32, name="result_0")
            result_1 = ring.tile([P, HALF], F32, name="result_1")
            if h == 0:
                rr_sb = ring.tile([P, HALF], F32, name="rr_sb")
                nc.scalar.copy(rr_sb[:], rr[:])
                nc.gpsimd.tensor_tensor(zr[:], rr_sb[:], ii_sb[:], SUB)
            else:
                nc.vector.tensor_tensor(zr[:], rr[:], ii_sb[:], SUB)
            gate = place([P, HALF], F32, "gate%d_%d" % (n, h), gate_at)
            nc.vector.tensor_copy(gate[:], gate_win[n][:].indirect(list_half(h)))
            rows, cols = slice(P * n, P * (n + 1)), slice(HALF * h, HALF * (h + 1))
            (nc.vector if last else nc.gpsimd).tensor_tensor(result_0[:], zr[:], gate[:], MULT)
            nc.sync.dma_start(out_0[rows, cols], result_0[:])
            nc.vector.tensor_tensor(result_1[:], ri[:], gate[:], MULT)
            nc.sync.dma_start(out_1[rows, cols], result_1[:])

        nc.sync.dma_start(offsets[:], offs)
        load_words(REAL, FIRST_TABLE_PIECES)
        load_table_scales(REAL)
        nc.sync.dma_start(wr4_sb[:].bitcast(I32), wr4_words.rearrange("a p b -> p a b").bitcast(I32))
        load_weight_scales(nc.gpsimd, wr4_sc, wr4_scales)
        nc.sync.dma_start(wi_sb[:], wi_words.rearrange("a p n i -> p a (n i)").bitcast(I32))
        load_table_scales(IMAG)
        load_words(IMAG, 1)
        load_weight_scales(nc.sync, wi_sc, wi_scales)

        parted_shape = [P, PASSES, 2 * HALF]
        picked_real = gather_words(REAL, 0, PICKED_REAL_AT)
        gather_scales(REAL, 0, FIRST_PLANES_AT)
        load_wrd(0, hold([P, PACK, N], F32, "wrd_raw0"))
        part_words(REAL, 0, picked_real, hold(parted_shape, U8, "parted_real0"))
        gather_scales(IMAG, 0, FIRST_PLANES_AT + HALF)
        load_wrd(1, place([P, PACK, N], F32, "wrd_raw1", II_AT))
        picked_imag = gather_words(IMAG, 0, PICKED_IMAG_AT)
        part_words(IMAG, 0, picked_imag, hold(parted_shape, U8, "parted_imag0"))
        load_gate_rows(0)
        load_gate_rows(1)

        gather_scales(REAL, 1, SECOND_REAL_PLANE_AT)
        picked_real = gather_words(REAL, 1, REAL_SCALES_AT)
        load_gate_rows(2)
        quantize_wrd(0, 0)
        part_words(REAL, 1, picked_real, place(parted_shape, U8, "parted_real1", grouped_at(0, 0)))
        quantize_wrd(0, 1)
        gather_scales(IMAG, 1, grouped_at(0, 1))
        quantize_wrd(1, 0)
        quantize_wrd(1, 1)
        picked_imag = gather_words(IMAG, 1, grouped_at(1, 1) + SLOT // 2)
        load_gate_rows(3)
        part_words(IMAG, 1, picked_imag, hold(parted_shape, U8, "parted_imag1"))

        for n in range(ROW_TILES):
            output_tile(n, 0, grouped_at(1, 1) - SLOT // 2 if n == 0 else GATES_AT + SLOT * n)
        for n in range(ROW_TILES):
            output_tile(n, 1, GATES_AT if n == ROW_TILES - 1 else II_AT + SLOT * n)
